import numpy as np
import ml_dtypes


def mxq(x, axis, fmt="e4m3"):
    dtype, down = {"e4m3": (ml_dtypes.float8_e4m3fn, 7), "e5m2": (ml_dtypes.float8_e5m2, 14)}[fmt]
    v = np.moveaxis(np.asarray(x, np.float32).astype(ml_dtypes.bfloat16).astype(np.float64), axis, -1)
    blocks = v.reshape(v.shape[:-1] + (-1, 32))
    amax = np.abs(blocks).max(-1, keepdims=True)
    byte = np.maximum(np.where(amax > 0, np.frexp(amax)[1] - 1 + 127, 0) - down, 1)
    scale = np.exp2(byte - 127.0)
    codes = (blocks / scale).astype(np.float32).astype(dtype).astype(np.float64)
    return np.moveaxis((codes * scale).reshape(v.shape), -1, axis)


WIDE = False


def mx_kscale(k):
    if not WIDE:
        return np.ones(k)
    levels = np.array([10, -10, 5, -5, 0])
    if k % 512:
        return np.exp2(np.random.permutation(np.resize(levels, k // 32))).repeat(32)
    a = np.empty((k // 512, 16))
    for p in range(k // 512):
        a[p, :8] = np.random.permutation(np.resize(levels, 8))
        for g in range(8):
            far = levels[np.abs(levels - a[p, g]) >= 10]
            a[p, g + 8] = far[np.random.randint(len(far))]
    return np.exp2(a.ravel()).repeat(32)


def f64(x):
    return np.asarray(x).astype(np.float64)


def striped(idx):
    return np.tile(idx.reshape(-1, 16).T, (8, 1)).astype(np.uint16)


def unstriped(offs):
    return offs[:16].T.reshape(-1).astype(np.int64)


E2M1 = np.array([0.0, 0.5, 1.0, 1.5, 2.0, 3.0, 4.0, 6.0, -0.0, -0.5, -1.0, -1.5, -2.0, -3.0, -4.0, -6.0])


def pack_weight(w, fmt):
    k, n = w.shape
    w = f64(np.asarray(w, np.float32).astype(ml_dtypes.bfloat16)).reshape(k // 32, 32, n)
    amax = np.abs(w).max(1)
    if fmt == "e4m3":
        byte = np.frexp(amax)[1] - 1 + 127 - 7
    else:
        mant, ex = np.frexp(amax / 6.0)
        byte = np.where(mant > 0.5, ex, ex - 1) + 127
    byte = np.clip(np.where(amax > 0, byte, 1), 1, 254)
    scaled = (w * np.exp2(127.0 - byte)[:, None, :]).reshape(k, n).astype(np.float32)
    by_word = np.ascontiguousarray(scaled.reshape(k // 512, 128, 4, n).transpose(0, 1, 3, 2))
    if fmt == "e4m3":
        words = by_word.astype(ml_dtypes.float8_e4m3fn).view(np.uint8)
    else:
        c = by_word.astype(ml_dtypes.float4_e2m1fn).view(np.uint8) & 0xF
        words = (c[..., 0::2] | (c[..., 1::2] << 4)).reshape(k // 512, 128, 2 * n)
    return np.ascontiguousarray(words), np.ascontiguousarray(byte.astype(np.uint8).reshape(k // 512, 16, n))


def unpack_weight(words, scales, fmt):
    g, _, n = scales.shape
    words = np.ascontiguousarray(words).reshape(g, 128, n, -1)
    if fmt == "e4m3":
        vals = words.view(ml_dtypes.float8_e4m3fn).astype(np.float64)
    else:
        nib = np.empty((g, 128, n, 4), np.uint8)
        nib[..., 0::2] = words & 0xF
        nib[..., 1::2] = words >> 4
        vals = E2M1[nib]
    vals = vals * np.repeat(np.exp2(scales.astype(np.float64) - 127.0), 8, axis=1)[..., None]
    return vals.transpose(0, 1, 3, 2).reshape(g * 512, n)


def relu(v):
    return np.maximum(v, 0.0)


K, T, E, C, N = 1536, 640, 6, 128, 256
TOP = 3
PAD = 64


def by_expert(wq, xq):
    return np.concatenate([wq[e].T @ xq[:, e * C:(e + 1) * C] for e in range(E)], axis=1)


def setup_inputs():
    n = np.random.standard_normal
    s = mx_kscale(K)[:, None]
    slot_token = np.empty(E * C, np.int64); pos = np.tile(E * C + np.arange(T) % PAD, (TOP, 1)); taken = np.zeros(T, np.int64)
    liked = np.random.randn(T)
    for e in np.random.permutation(E):
        free = np.flatnonzero(taken < TOP); pick = np.random.permutation(free[np.argsort(-(liked[free] + np.random.gumbel(size=free.size)))[:C]]); slot_token[e * C:(e + 1) * C] = pick
        pos[taken[pick], pick] = e * C + np.arange(C); taken[pick] += 1
    g = np.random.uniform(0.2, 0.8, (TOP, T))
    w = [pack_weight(m, "e2m1") for m in n((E, K, N)) / np.sqrt(K) / s[None]]
    return {
        "xT": (n((K, T)) * s).astype(np.float32),
        "w_words": np.stack([m[0] for m in w]),
        "w_scales": np.stack([m[1] for m in w]),
        "b": (0.3 * n((N, E))).astype(np.float32),
        "gate": np.stack([np.tile(r, (N, 1)) for r in g]).astype(np.float32),
        "offs": striped(slot_token),
        "pos1": striped(pos[0]),
        "pos2": striped(pos[1]),
        "pos3": striped(pos[2]),
    }


def reference(xT, w_words, w_scales, b, gate, offs, pos1, pos2, pos3):
    idx = unstriped(offs)
    w = np.stack([unpack_weight(w_words[e], w_scales[e], "e2m1") for e in range(E)])
    xq = mxq(f64(xT)[:, idx], 0, "e4m3")
    y = by_expert(w, xq)
    y = relu(y + np.repeat(f64(b), C, axis=1))
    y = np.concatenate([y, np.zeros((N, PAD))], axis=1)
    return sum(f64(gate[r]) * y[:, unstriped(p)] for r, p in enumerate((pos1, pos2, pos3)))

@@ -1,0 +1,203 @@
+from contextlib import ExitStack
+
+import concourse.mybir as mybir
+
+K, T, E, C, N = 1536, 640, 6, 128, 256
+TOP, PAD = 3, 64
+S = E * C
+P = 128
+PACK = 4
+PASSES = K // (P * PACK)
+HALVES = N // P
+FLOPS = 2 * K * N * S
+
+F32 = mybir.dt.float32
+BF16 = mybir.dt.bfloat16
+I32 = mybir.dt.int32
+U32 = mybir.dt.uint32
+U16 = mybir.dt.uint16
+U8 = mybir.dt.uint8
+FP8X4 = mybir.dt.float8_e4m3fn_x4
+FP4X4 = mybir.dt.float4_e2m1fn_x4
+ACT = mybir.ActivationFunctionType
+ALU = mybir.AluOpType
+
+X_CHUNKS = (
+    ((0, 128, 48), (128, 384, 208), (384, 640, 464)),
+    ((0, 256, 256), (256, 512, 448), (512, 640, 512)),
+    ((0, 320, 320), (320, 640, 640)),
+)
+Q_CHUNKS = (
+    ((0, 128), (128, 384), (384, 640)),
+    ((0, 512), (512, 640)),
+    ((0, 512), (512, 640)),
+)
+SHIFT_ROWS = 112
+
+
+def tile_moe_ecr_lin_relu_kernel(
+    tc, xT, w_words, w_scales, b, gate, offs, pos1, pos2, pos3, out
+):
+    nc = tc.nc
+    with ExitStack() as ctx:
+        keep = ctx.enter_context(tc.tile_pool(name="keep", bufs=1))
+        psum = ctx.enter_context(tc.psum_pool(name="psum", bufs=1))
+
+        slot_list = keep.tile([P, S // 16], U16, name="slot_list")
+        pos_lists = [keep.tile([P, T // 16], U16, name=f"pos_list{r}") for r in range(TOP)]
+        w_codes = [keep.tile([P, E, 2 * N], U8, name=f"w_codes{a}", align_bytes=64) for a in range(PASSES)]
+        w_plane = keep.tile([P, E * PASSES, N], U8, name="w_plane", align_bytes=64)
+        bias = keep.tile([P, HALVES, 8], F32, name="bias")
+        gates = [[keep.tile([P, T], F32, name=f"gate{h}_{r}") for r in range(TOP)] for h in range(HALVES)]
+        x_bf = [keep.tile([P, T, PACK], BF16, name=f"x_bf{a}", align_bytes=64) for a in range(PASSES)]
+        tok_words = [keep.tile([P, T], U32, name=f"tok_words{a}", align_bytes=64) for a in range(PASSES)]
+        tok_bytes01 = keep.tile([P, T], U8, name="tok_bytes01", align_bytes=64)
+        tok_bytes2 = keep.tile([P, T], U8, name="tok_bytes2", align_bytes=64)
+        slot_words = [keep.tile([P, S], U32, name=f"slot_words{a}", align_bytes=64) for a in range(PASSES)]
+        slot_bytes = [keep.tile([P, S], U8, name=f"slot_bytes{a}", align_bytes=64) for a in range(PASSES)]
+        y = [keep.tile([P, S + PAD], F32, name=f"y{h}") for h in range(HALVES)]
+        zeros = keep.tile([P, PAD], F32, name="zeros")
+        prods = [[keep.tile([P, T], F32, name=f"prod{h}_{r}") for r in range(TOP)] for h in range(HALVES)]
+        part = [keep.tile([P, T], F32, name=f"part{h}") for h in range(HALVES)]
+        res = [keep.tile([P, T], F32, name=f"res{h}") for h in range(HALVES)]
+
+        nc.vector.memset(zeros[:], 0.0)
+        for h in range(HALVES):
+            nc.scalar.activation(y[h][:, S:], zeros[:], ACT.Relu)
+        nc.vector.memset(tok_bytes01[:].bitcast(I32), 0)
+        nc.vector.memset(tok_bytes2[:].bitcast(I32), 0)
+        nc.vector.memset(slot_bytes[1][:].bitcast(I32), 0)
+        nc.vector.memset(w_plane[:].rearrange("p g n -> p (g n)").bitcast(I32), 0)
+
+        raw = {}
+        for a in range(PASSES):
+            rows = xT[a * P * PACK : (a + 1) * P * PACK, :].rearrange("(p j) t -> p j t", j=PACK)
+            for t0, t1, split in X_CHUNKS[a]:
+                raw[a, t0] = keep.tile([P, PACK, t1 - t0], F32, name=f"raw{a}_{t0}")
+                nc.sync.dma_start(out=raw[a, t0][:], in_=rows[:, :, t0:t1])
+            if a == 0:
+                nc.sync.dma_start(slot_list[:], offs)
+        for q in range(4):
+            nc.sync.dma_start(
+                out=w_plane[32 * q : 32 * q + 4, :, :].bitcast(I32),
+                in_=w_scales[:, :, 4 * q : 4 * q + 4, :].rearrange("e a q n -> q (e a) n").bitcast(I32),
+            )
+        nc.sync.dma_start(out=bias[:, :, 0:E], in_=b.rearrange("(h p) e -> p h e", p=P))
+        for a in range(PASSES):
+            nc.sync.dma_start(
+                out=w_codes[a][:].bitcast(I32),
+                in_=w_words[:, a, :, :].rearrange("e p c -> p e c").bitcast(I32),
+            )
+        for r, pos in enumerate((pos1, pos2, pos3)):
+            nc.sync.dma_start(pos_lists[r][:], pos)
+        for h in range(HALVES):
+            for r in range(TOP):
+                nc.sync.dma_start(out=gates[h][r][:], in_=gate[r, h * P : (h + 1) * P, :])
+
+        def cast(a):
+            for t0, t1, split in X_CHUNKS[a]:
+                for eng, lo, hi in (("s", t0, split), ("v", split, t1)):
+                    if hi > lo:
+                        dst = x_bf[a][:, lo:hi, :].rearrange("p (c i) j -> p c j i", i=4)
+                        src = raw[a, t0][:, :, lo - t0 : hi - t0].rearrange("p j (c i) -> p c j i", i=4)
+                        if eng == "s":
+                            nc.scalar.activation(dst, src, ACT.Copy)
+                        else:
+                            nc.vector.tensor_copy(dst, src)
+
+        def quantize(a):
+            for t0, t1 in Q_CHUNKS[a]:
+                plane = (tok_bytes01[:, t0:t1], tok_bytes01[4:, t0:t1], tok_bytes2[:, t0:t1])[a]
+                nc.vector.quantize_mx(
+                    out=tok_words[a][:, t0:t1].bitcast(FP8X4),
+                    scales=plane,
+                    in_=x_bf[a][:, t0:t1, :].rearrange("p t j -> p (t j)"),
+                )
+
+        def gather(dst, window, e0, e1):
+            nc.vector.tensor_copy(
+                dst[:, e0 * C : e1 * C], window[:].indirect(slot_list[:, e0 * C // 16 : e1 * C // 16])
+            )
+
+        acc = {}
+
+        def multiply(e, h, a):
+            if a == 0:
+                acc[e, h] = psum.tile([P, C], F32, name=f"acc{e}_{h}", tag=f"bank{(h * E + e) % 8}")
+            cols = slice(e * C, (e + 1) * C)
+            nc.tensor.matmul_mx(
+                out=acc[e, h][:],
+                lhsT=w_codes[a][:, e, h * 2 * P : (h + 1) * 2 * P].bitcast(FP4X4),
+                lhsT_scale=w_plane[:, e * PASSES + a, h * P : (h + 1) * P],
+                rhs=slot_words[a][:, cols].bitcast(FP8X4),
+                rhs_scale=slot_bytes[a][:, cols],
+                start=(a == 0),
+                stop=(a == PASSES - 1),
+            )
+
+        def activate(e, h):
+            nc.scalar.activation(
+                y[h][:, e * C : (e + 1) * C], acc[e, h][:], ACT.Relu, bias=bias[:, h, e : e + 1]
+            )
+
+        early = [(e, 0) for e in range(E)] + [(0, 1), (1, 1)]
+        late = [(e, 1) for e in range(2, E)]
+
+        cast(0)
+        quantize(0)
+        for e0, e1 in ((0, 3), (3, 6)):
+            gather(slot_words[0], tok_words[0], e0, e1)
+        cast(1)
+        quantize(1)
+        for e0, e1 in ((0, 3), (3, 6)):
+            gather(slot_bytes[0], tok_bytes01, e0, e1)
+        for e0, e1 in ((0, 3), (3, 6)):
+            gather(slot_words[1], tok_words[1], e0, e1)
+        cast(2)
+        nc.scalar.dma_start(
+            out=slot_bytes[1][0:SHIFT_ROWS, :].bitcast(I32),
+            in_=slot_bytes[0][4 : 4 + SHIFT_ROWS, :].bitcast(I32),
+        )
+        quantize(2)
+        for a in range(PASSES - 1):
+            for e, h in early:
+                multiply(e, h, a)
+        for e0, e1 in ((0, 3), (3, 5), (5, 6)):
+            gather(slot_words[2], tok_words[2], e0, e1)
+            gather(slot_bytes[2], tok_bytes2, e0, e1)
+            for e in range(e0, e1):
+                multiply(e, 0, 2)
+                activate(e, 0)
+        for e in range(2):
+            multiply(e, 1, 2)
+            activate(e, 1)
+        for e, h in late:
+            for a in range(PASSES):
+                multiply(e, h, a)
+            activate(e, h)
+
+        def fetch(h, r, t0, t1):
+            nc.vector.tensor_tensor(
+                prods[h][r][:, t0:t1],
+                y[h][:].indirect(pos_lists[r][:, t0 // 16 : t1 // 16]),
+                gates[h][r][:, t0:t1],
+                ALU.mult,
+            )
+
+        def add_first(h, t0, t1):
+            nc.vector.tensor_tensor(part[h][:, t0:t1], prods[h][0][:, t0:t1], prods[h][1][:, t0:t1], ALU.add)
+
+        def finish(h, t0, t1):
+            nc.vector.tensor_tensor(res[h][:, t0:t1], part[h][:, t0:t1], prods[h][2][:, t0:t1], ALU.add)
+            nc.sync.dma_start(out=out[h * P : (h + 1) * P, t0:t1], in_=res[h][:, t0:t1])
+
+        pieces = ((0, 0, T), (1, 0, 384), (1, 384, T))
+        for i, piece in enumerate(pieces):
+            h, t0, t1 = piece
+            fetch(h, 0, t0, t1)
+            if i > 0:
+                finish(*pieces[i - 1])
+            fetch(h, 1, t0, t1)
+            fetch(h, 2, t0, t1)
+            add_first(h, t0, t1)
+        finish(*pieces[-1])

@@ -1,6 +1,7 @@
 from contextlib import ExitStack
 
 import concourse.mybir as mybir
+from concourse.masks import make_identity
 
 K, T, E, C, N = 1536, 640, 6, 128, 256
 TOP, PAD = 3, 64
@@ -23,16 +24,16 @@ ACT = mybir.ActivationFunctionType
 ALU = mybir.AluOpType
 
 X_CHUNKS = (
-    ((0, 128, 48), (128, 384, 208), (384, 640, 464)),
-    ((0, 256, 256), (256, 512, 448), (512, 640, 512)),
-    ((0, 320, 320), (320, 640, 640)),
+    ((0, 256, 96), (256, 512, 352), (512, 640, 560)),
+    ((0, 256, 256), (256, 512, 384), (512, 640, 560)),
+    ((0, 256, 256), (256, 512, 512), (512, 640, 640)),
 )
 Q_CHUNKS = (
-    ((0, 128), (128, 384), (384, 640)),
-    ((0, 512), (512, 640)),
+    ((0, 256), (256, 512), (512, 640)),
+    ((0, 256), (256, 512), (512, 640)),
     ((0, 512), (512, 640)),
 )
-SHIFT_ROWS = 112
+SHIFT_ROWS = ((0, 64), (64, 68), (96, 100))
 
 
 def tile_moe_ecr_lin_relu_kernel(
@@ -48,7 +49,6 @@ def tile_moe_ecr_lin_relu_kernel(
         w_codes = [keep.tile([P, E, 2 * N], U8, name=f"w_codes{a}", align_bytes=64) for a in range(PASSES)]
         w_plane = keep.tile([P, E * PASSES, N], U8, name="w_plane", align_bytes=64)
         bias = keep.tile([P, HALVES, 8], F32, name="bias")
-        gates = [[keep.tile([P, T], F32, name=f"gate{h}_{r}") for r in range(TOP)] for h in range(HALVES)]
         x_bf = [keep.tile([P, T, PACK], BF16, name=f"x_bf{a}", align_bytes=64) for a in range(PASSES)]
         tok_words = [keep.tile([P, T], U32, name=f"tok_words{a}", align_bytes=64) for a in range(PASSES)]
         tok_bytes01 = keep.tile([P, T], U8, name="tok_bytes01", align_bytes=64)
@@ -58,41 +58,40 @@ def tile_moe_ecr_lin_relu_kernel(
         y = [keep.tile([P, S + PAD], F32, name=f"y{h}") for h in range(HALVES)]
         zeros = keep.tile([P, PAD], F32, name="zeros")
         prods = [[keep.tile([P, T], F32, name=f"prod{h}_{r}") for r in range(TOP)] for h in range(HALVES)]
-        part = [keep.tile([P, T], F32, name=f"part{h}") for h in range(HALVES)]
+        turned = [keep.tile([P, T], F32, name=f"turned{h}") for h in range(HALVES)]
+        ident = keep.tile([P, P], F32, name="ident")
         res = [keep.tile([P, T], F32, name=f"res{h}") for h in range(HALVES)]
 
         nc.vector.memset(zeros[:], 0.0)
+        nc.vector.memset(w_plane[:].rearrange("p g n -> p (g n)").bitcast(I32), 0)
+        make_identity(nc, ident[:])
         for h in range(HALVES):
             nc.scalar.activation(y[h][:, S:], zeros[:], ACT.Relu)
         nc.vector.memset(tok_bytes01[:].bitcast(I32), 0)
         nc.vector.memset(tok_bytes2[:].bitcast(I32), 0)
         nc.vector.memset(slot_bytes[1][:].bitcast(I32), 0)
-        nc.vector.memset(w_plane[:].rearrange("p g n -> p (g n)").bitcast(I32), 0)
 
         raw = {}
         for a in range(PASSES):
             rows = xT[a * P * PACK : (a + 1) * P * PACK, :].rearrange("(p j) t -> p j t", j=PACK)
             for t0, t1, split in X_CHUNKS[a]:
-                raw[a, t0] = keep.tile([P, PACK, t1 - t0], F32, name=f"raw{a}_{t0}")
+                raw[a, t0] = keep.tile([P, PACK, t1 - t0], F32, name=f"raw{a}_{t0}", align_bytes=64)
                 nc.sync.dma_start(out=raw[a, t0][:], in_=rows[:, :, t0:t1])
             if a == 0:
                 nc.sync.dma_start(slot_list[:], offs)
         for q in range(4):
-            nc.sync.dma_start(
+            nc.gpsimd.dma_start(
                 out=w_plane[32 * q : 32 * q + 4, :, :].bitcast(I32),
                 in_=w_scales[:, :, 4 * q : 4 * q + 4, :].rearrange("e a q n -> q (e a) n").bitcast(I32),
             )
-        nc.sync.dma_start(out=bias[:, :, 0:E], in_=b.rearrange("(h p) e -> p h e", p=P))
-        for a in range(PASSES):
-            nc.sync.dma_start(
-                out=w_codes[a][:].bitcast(I32),
-                in_=w_words[:, a, :, :].rearrange("e p c -> p e c").bitcast(I32),
-            )
+        nc.scalar.dma_start(out=bias[:, :, 0:E], in_=b.rearrange("(h p) e -> p h e", p=P))
         for r, pos in enumerate((pos1, pos2, pos3)):
             nc.sync.dma_start(pos_lists[r][:], pos)
-        for h in range(HALVES):
-            for r in range(TOP):
-                nc.sync.dma_start(out=gates[h][r][:], in_=gate[r, h * P : (h + 1) * P, :])
+        for a, e0, e1 in ((0, 0, E), (1, 0, E), (2, 0, 3), (2, 3, E)):
+            nc.sync.dma_start(
+                out=w_codes[a][:, e0:e1, :].bitcast(I32),
+                in_=w_words[e0:e1, a, :, :].rearrange("e p c -> p e c").bitcast(I32),
+            )
 
         def cast(a):
             for t0, t1, split in X_CHUNKS[a]:
@@ -154,10 +153,11 @@ def tile_moe_ecr_lin_relu_kernel(
         for e0, e1 in ((0, 3), (3, 6)):
             gather(slot_words[1], tok_words[1], e0, e1)
         cast(2)
-        nc.scalar.dma_start(
-            out=slot_bytes[1][0:SHIFT_ROWS, :].bitcast(I32),
-            in_=slot_bytes[0][4 : 4 + SHIFT_ROWS, :].bitcast(I32),
-        )
+        for p0, p1 in SHIFT_ROWS:
+            nc.scalar.dma_start(
+                out=slot_bytes[1][p0:p1, :].bitcast(I32),
+                in_=slot_bytes[0][p0 + 4 : p1 + 4, :].bitcast(I32),
+            )
         quantize(2)
         for a in range(PASSES - 1):
             for e, h in early:
@@ -176,28 +176,60 @@ def tile_moe_ecr_lin_relu_kernel(
                 multiply(e, h, a)
             activate(e, h)
 
+        gates = {}
+        spent = ("raw2_0", "raw2_256", "tok_words1", "raw2_512", "x_bf2", "tok_words2")
+        for i, tag in enumerate(spent):
+            h, r = divmod(i, TOP)
+            gates[h, r] = keep.tile([P, T], F32, name=f"gate{h}_{r}", tag=tag, align_bytes=64)
+            nc.sync.dma_start(out=gates[h, r][:], in_=gate[r, h * P : (h + 1) * P, :])
+
         def fetch(h, r, t0, t1):
             nc.vector.tensor_tensor(
                 prods[h][r][:, t0:t1],
                 y[h][:].indirect(pos_lists[r][:, t0 // 16 : t1 // 16]),
-                gates[h][r][:, t0:t1],
+                gates[h, r][:, t0:t1],
                 ALU.mult,
             )
 
-        def add_first(h, t0, t1):
-            nc.vector.tensor_tensor(part[h][:, t0:t1], prods[h][0][:, t0:t1], prods[h][1][:, t0:t1], ALU.add)
+        blocks = T // P
+        sums = {}
 
-        def finish(h, t0, t1):
-            nc.vector.tensor_tensor(res[h][:, t0:t1], part[h][:, t0:t1], prods[h][2][:, t0:t1], ALU.add)
-            nc.sync.dma_start(out=out[h * P : (h + 1) * P, t0:t1], in_=res[h][:, t0:t1])
+        def turn_add(h, r, last):
+            for i in range(blocks):
+                if r == 0:
+                    sums[h, i] = psum.tile([P, P], F32, name=f"sum{h}_{i}", tag=f"bank{(4 + i) % 8}")
+                nc.tensor.matmul(
+                    sums[h, i][:], prods[h][r][:, i * P : (i + 1) * P], ident[:],
+                    start=(r == 0), stop=last, is_transpose=True,
+                )
+                if last:
+                    nc.scalar.activation(turned[h][:, i * P : (i + 1) * P], sums[h, i][:], ACT.Copy)
 
-        pieces = ((0, 0, T), (1, 0, 384), (1, 384, T))
-        for i, piece in enumerate(pieces):
-            h, t0, t1 = piece
-            fetch(h, 0, t0, t1)
-            if i > 0:
-                finish(*pieces[i - 1])
-            fetch(h, 1, t0, t1)
-            fetch(h, 2, t0, t1)
-            add_first(h, t0, t1)
-        finish(*pieces[-1])
+        pieces = ((0, 384), (384, T))
+
+        def turn_back(h):
+            back = []
+            for k, (t0, t1) in enumerate(pieces):
+                bank = psum.tile([P, t1 - t0], F32, name=f"back{h}_{k}", tag=f"bank{1 + k}")
+                for i in range(t0 // P, t1 // P):
+                    nc.tensor.transpose(bank[:, i * P - t0 : (i + 1) * P - t0], turned[h][:, i * P : (i + 1) * P], ident[:])
+                back.append(bank)
+            return back
+
+        for r in range(TOP):
+            fetch(0, r, 0, T)
+            turn_add(0, r, r == TOP - 1)
+        back = turn_back(0)
+        for k, (t0, t1) in enumerate(pieces):
+            nc.scalar.activation(res[0][:, t0:t1], back[k][:], ACT.Copy)
+        nc.sync.dma_start(out=out[0:P, :], in_=res[0][:])
+
+        for r in range(TOP - 1):
+            fetch(1, r, 0, T)
+            turn_add(1, r, r == TOP - 2)
+        back = turn_back(1)
+        for t0, t1 in pieces:
+            fetch(1, TOP - 1, t0, t1)
+        for k, (t0, t1) in enumerate(pieces):
+            nc.vector.tensor_tensor(res[1][:, t0:t1], prods[1][TOP - 1][:, t0:t1], back[k][:], ALU.add)
+            nc.sync.dma_start(out=out[P : 2 * P, t0:t1], in_=res[1][:, t0:t1])

@@ -24,15 +24,21 @@ ACT = mybir.ActivationFunctionType
 ALU = mybir.AluOpType
 
 X_CHUNKS = (
-    ((0, 256, 96), (256, 512, 352), (512, 640, 560)),
-    ((0, 256, 256), (256, 512, 384), (512, 640, 560)),
-    ((0, 256, 256), (256, 512, 512), (512, 640, 640)),
+    ((0, 640),),
+    ((0, 256), (256, 512), (512, 640)),
+    ((0, 256), (256, 512), (512, 640)),
+)
+CASTS = (
+    (("s", 0, 0, 256), ("v", 0, 256, 512), ("v", 0, 512, 640)),
+    (("s", 0, 0, 256), ("s", 256, 256, 512), ("v", 512, 512, 640)),
+    (("s", 0, 0, 256), ("s", 256, 256, 512), ("s", 512, 512, 640)),
 )
 Q_CHUNKS = (
-    ((0, 256), (256, 512), (512, 640)),
+    ((256, 512), (512, 640), (0, 256)),
     ((0, 256), (256, 512), (512, 640)),
     ((0, 512), (512, 640)),
 )
+ORDER = (2, 1, 0)
 SHIFT_ROWS = ((0, 64), (64, 68), (96, 100))
 
 
@@ -46,7 +52,6 @@ def tile_moe_ecr_lin_relu_kernel(
 
         slot_list = keep.tile([P, S // 16], U16, name="slot_list")
         pos_lists = [keep.tile([P, T // 16], U16, name=f"pos_list{r}") for r in range(TOP)]
-        w_codes = [keep.tile([P, E, 2 * N], U8, name=f"w_codes{a}", align_bytes=64) for a in range(PASSES)]
         w_plane = keep.tile([P, E * PASSES, N], U8, name="w_plane", align_bytes=64)
         bias = keep.tile([P, HALVES, 8], F32, name="bias")
         x_bf = [keep.tile([P, T, PACK], BF16, name=f"x_bf{a}", align_bytes=64) for a in range(PASSES)]
@@ -74,35 +79,43 @@ def tile_moe_ecr_lin_relu_kernel(
         raw = {}
         for a in range(PASSES):
             rows = xT[a * P * PACK : (a + 1) * P * PACK, :].rearrange("(p j) t -> p j t", j=PACK)
-            for t0, t1, split in X_CHUNKS[a]:
+            for t0, t1 in X_CHUNKS[a]:
                 raw[a, t0] = keep.tile([P, PACK, t1 - t0], F32, name=f"raw{a}_{t0}", align_bytes=64)
                 nc.sync.dma_start(out=raw[a, t0][:], in_=rows[:, :, t0:t1])
             if a == 0:
                 nc.sync.dma_start(slot_list[:], offs)
+        nc.scalar.dma_start(out=bias[:, :, 0:E], in_=b.rearrange("(h p) e -> p h e", p=P))
+        for r, pos in enumerate((pos1, pos2, pos3)):
+            nc.sync.dma_start(pos_lists[r][:], pos)
         for q in range(4):
             nc.gpsimd.dma_start(
                 out=w_plane[32 * q : 32 * q + 4, :, :].bitcast(I32),
                 in_=w_scales[:, :, 4 * q : 4 * q + 4, :].rearrange("e a q n -> q (e a) n").bitcast(I32),
             )
-        nc.scalar.dma_start(out=bias[:, :, 0:E], in_=b.rearrange("(h p) e -> p h e", p=P))
-        for r, pos in enumerate((pos1, pos2, pos3)):
-            nc.sync.dma_start(pos_lists[r][:], pos)
-        for a, e0, e1 in ((0, 0, E), (1, 0, E), (2, 0, 3), (2, 3, E)):
+        w_codes = {}
+
+        def load_weights(a, e0, e1, tag):
+            codes = keep.tile([P, e1 - e0, 2 * N], U8, name=f"w_codes{a}_{e0}", tag=tag, align_bytes=64)
             nc.sync.dma_start(
-                out=w_codes[a][:, e0:e1, :].bitcast(I32),
+                out=codes[:].bitcast(I32),
                 in_=w_words[e0:e1, a, :, :].rearrange("e p c -> p e c").bitcast(I32),
             )
+            for e in range(e0, e1):
+                w_codes[e, a] = codes[:, e - e0, :]
+
+        load_weights(0, 0, E, "w_codes0")
+        load_weights(1, 0, E, "w_codes1")
+        load_weights(2, 0, 3, "w_codes2a")
+        load_weights(2, 3, E, "w_codes2b")
 
         def cast(a):
-            for t0, t1, split in X_CHUNKS[a]:
-                for eng, lo, hi in (("s", t0, split), ("v", split, t1)):
-                    if hi > lo:
-                        dst = x_bf[a][:, lo:hi, :].rearrange("p (c i) j -> p c j i", i=4)
-                        src = raw[a, t0][:, :, lo - t0 : hi - t0].rearrange("p j (c i) -> p c j i", i=4)
-                        if eng == "s":
-                            nc.scalar.activation(dst, src, ACT.Copy)
-                        else:
-                            nc.vector.tensor_copy(dst, src)
+            for eng, t0, lo, hi in CASTS[a]:
+                dst = x_bf[a][:, lo:hi, :].rearrange("p (c i) j -> p c j i", i=4)
+                src = raw[a, t0][:, :, lo - t0 : hi - t0].rearrange("p j (c i) -> p c j i", i=4)
+                if eng == "s":
+                    nc.scalar.activation(dst, src, ACT.Copy)
+                else:
+                    nc.vector.tensor_copy(dst, src)
 
         def quantize(a):
             for t0, t1 in Q_CHUNKS[a]:
@@ -126,7 +139,7 @@ def tile_moe_ecr_lin_relu_kernel(
             cols = slice(e * C, (e + 1) * C)
             nc.tensor.matmul_mx(
                 out=acc[e, h][:],
-                lhsT=w_codes[a][:, e, h * 2 * P : (h + 1) * 2 * P].bitcast(FP4X4),
+                lhsT=w_codes[e, a][:, h * 2 * P : (h + 1) * 2 * P].bitcast(FP4X4),
                 lhsT_scale=w_plane[:, e * PASSES + a, h * P : (h + 1) * P],
                 rhs=slot_words[a][:, cols].bitcast(FP8X4),
                 rhs_scale=slot_bytes[a][:, cols],
@@ -179,7 +192,7 @@ def tile_moe_ecr_lin_relu_kernel(
         gates = {}
         spent = ("raw2_0", "raw2_256", "tok_words1", "raw2_512", "x_bf2", "tok_words2")
         for i, tag in enumerate(spent):
-            h, r = divmod(i, TOP)
+            h, r = i // TOP, ORDER[i % TOP]
             gates[h, r] = keep.tile([P, T], F32, name=f"gate{h}_{r}", tag=tag, align_bytes=64)
             nc.sync.dma_start(out=gates[h, r][:], in_=gate[r, h * P : (h + 1) * P, :])
 
@@ -196,11 +209,11 @@ def tile_moe_ecr_lin_relu_kernel(
 
         def turn_add(h, r, last):
             for i in range(blocks):
-                if r == 0:
+                if r == ORDER[0]:
                     sums[h, i] = psum.tile([P, P], F32, name=f"sum{h}_{i}", tag=f"bank{(4 + i) % 8}")
                 nc.tensor.matmul(
                     sums[h, i][:], prods[h][r][:, i * P : (i + 1) * P], ident[:],
-                    start=(r == 0), stop=last, is_transpose=True,
+                    start=(r == ORDER[0]), stop=last, is_transpose=True,
                 )
                 if last:
                     nc.scalar.activation(turned[h][:, i * P : (i + 1) * P], sums[h, i][:], ACT.Copy)
@@ -216,20 +229,19 @@ def tile_moe_ecr_lin_relu_kernel(
                 back.append(bank)
             return back
 
-        for r in range(TOP):
+        for r in ORDER:
             fetch(0, r, 0, T)
-            turn_add(0, r, r == TOP - 1)
+            turn_add(0, r, r == ORDER[-1])
         back = turn_back(0)
         for k, (t0, t1) in enumerate(pieces):
             nc.scalar.activation(res[0][:, t0:t1], back[k][:], ACT.Copy)
         nc.sync.dma_start(out=out[0:P, :], in_=res[0][:])
 
-        for r in range(TOP - 1):
-            fetch(1, r, 0, T)
-            turn_add(1, r, r == TOP - 2)
-        back = turn_back(1)
+        fetch(1, ORDER[0], 0, T)
+        fetch(1, ORDER[1], 0, T)
+        fetch(1, ORDER[2], *pieces[0])
+        nc.vector.tensor_tensor(turned[1][:], prods[1][ORDER[0]][:], prods[1][ORDER[1]][:], ALU.add)
+        fetch(1, ORDER[2], *pieces[1])
         for t0, t1 in pieces:
-            fetch(1, TOP - 1, t0, t1)
-        for k, (t0, t1) in enumerate(pieces):
-            nc.vector.tensor_tensor(res[1][:, t0:t1], prods[1][TOP - 1][:, t0:t1], back[k][:], ALU.add)
+            nc.vector.tensor_tensor(res[1][:, t0:t1], prods[1][ORDER[2]][:, t0:t1], turned[1][:, t0:t1], ALU.add)
             nc.sync.dma_start(out=out[P : 2 * P, t0:t1], in_=res[1][:, t0:t1])

@@ -30,7 +30,7 @@ X_CHUNKS = (
 )
 CASTS = (
     (("s", 0, 0, 256), ("v", 0, 256, 512), ("v", 0, 512, 640)),
-    (("s", 0, 0, 256), ("s", 256, 256, 512), ("v", 512, 512, 640)),
+    (("s", 0, 0, 256), ("s", 256, 256, 512), ("s", 512, 512, 640)),
     (("s", 0, 0, 256), ("s", 256, 256, 512), ("s", 512, 512, 640)),
 )
 Q_CHUNKS = (
@@ -39,7 +39,8 @@ Q_CHUNKS = (
     ((0, 512), (512, 640)),
 )
 ORDER = (2, 1, 0)
-SHIFT_ROWS = ((0, 64), (64, 68), (96, 100))
+WIDE = 1024
+SHIFT_ROWS = ((0, 112),)
 
 
 def tile_moe_ecr_lin_relu_kernel(
@@ -55,8 +56,8 @@ def tile_moe_ecr_lin_relu_kernel(
         w_plane = keep.tile([P, E * PASSES, N], U8, name="w_plane", align_bytes=64)
         bias = keep.tile([P, HALVES, 8], F32, name="bias")
         x_bf = [keep.tile([P, T, PACK], BF16, name=f"x_bf{a}", align_bytes=64) for a in range(PASSES)]
-        tok_words = [keep.tile([P, T], U32, name=f"tok_words{a}", align_bytes=64) for a in range(PASSES)]
-        tok_bytes01 = keep.tile([P, T], U8, name="tok_bytes01", align_bytes=64)
+        tok_words = [keep.tile([P, (WIDE, WIDE, T)[a]], U32, name=f"tok_words{a}", align_bytes=64) for a in range(PASSES)]
+        tok_bytes01 = keep.tile([P, WIDE], U8, name="tok_bytes01", align_bytes=64)
         tok_bytes2 = keep.tile([P, T], U8, name="tok_bytes2", align_bytes=64)
         slot_words = [keep.tile([P, S], U32, name=f"slot_words{a}", align_bytes=64) for a in range(PASSES)]
         slot_bytes = [keep.tile([P, S], U8, name=f"slot_bytes{a}", align_bytes=64) for a in range(PASSES)]
@@ -74,6 +75,8 @@ def tile_moe_ecr_lin_relu_kernel(
             nc.scalar.activation(y[h][:, S:], zeros[:], ACT.Relu)
         nc.vector.memset(tok_bytes01[:].bitcast(I32), 0)
         nc.vector.memset(tok_bytes2[:].bitcast(I32), 0)
+        for a in range(PASSES - 1):
+            nc.vector.memset(tok_words[a][:, T:].bitcast(I32), 0)
         nc.vector.memset(slot_bytes[1][:].bitcast(I32), 0)
 
         raw = {}
@@ -84,14 +87,12 @@ def tile_moe_ecr_lin_relu_kernel(
                 nc.sync.dma_start(out=raw[a, t0][:], in_=rows[:, :, t0:t1])
             if a == 0:
                 nc.sync.dma_start(slot_list[:], offs)
-        nc.scalar.dma_start(out=bias[:, :, 0:E], in_=b.rearrange("(h p) e -> p h e", p=P))
-        for r, pos in enumerate((pos1, pos2, pos3)):
-            nc.sync.dma_start(pos_lists[r][:], pos)
         for q in range(4):
-            nc.gpsimd.dma_start(
+            nc.sync.dma_start(
                 out=w_plane[32 * q : 32 * q + 4, :, :].bitcast(I32),
                 in_=w_scales[:, :, 4 * q : 4 * q + 4, :].rearrange("e a q n -> q (e a) n").bitcast(I32),
             )
+        nc.sync.dma_start(out=bias[:, :, 0:E], in_=b.rearrange("(h p) e -> p h e", p=P))
         w_codes = {}
 
         def load_weights(a, e0, e1, tag):
@@ -105,8 +106,8 @@ def tile_moe_ecr_lin_relu_kernel(
 
         load_weights(0, 0, E, "w_codes0")
         load_weights(1, 0, E, "w_codes1")
-        load_weights(2, 0, 3, "w_codes2a")
-        load_weights(2, 3, E, "w_codes2b")
+        for r in ORDER:
+            nc.sync.dma_start(pos_lists[r][:], (pos1, pos2, pos3)[r])
 
         def cast(a):
             for eng, t0, lo, hi in CASTS[a]:
@@ -157,20 +158,19 @@ def tile_moe_ecr_lin_relu_kernel(
 
         cast(0)
         quantize(0)
-        for e0, e1 in ((0, 3), (3, 6)):
-            gather(slot_words[0], tok_words[0], e0, e1)
+        gather(slot_words[0], tok_words[0], 0, E)
         cast(1)
         quantize(1)
-        for e0, e1 in ((0, 3), (3, 6)):
-            gather(slot_bytes[0], tok_bytes01, e0, e1)
-        for e0, e1 in ((0, 3), (3, 6)):
-            gather(slot_words[1], tok_words[1], e0, e1)
+        gather(slot_bytes[0], tok_bytes01, 0, E)
+        gather(slot_words[1], tok_words[1], 0, E)
         cast(2)
         for p0, p1 in SHIFT_ROWS:
             nc.scalar.dma_start(
                 out=slot_bytes[1][p0:p1, :].bitcast(I32),
                 in_=slot_bytes[0][p0 + 4 : p1 + 4, :].bitcast(I32),
             )
+        load_weights(2, 0, 3, "tok_bytes01")
+        load_weights(2, 3, E, "raw2_256")
         quantize(2)
         for a in range(PASSES - 1):
             for e, h in early:
@@ -190,7 +190,7 @@ def tile_moe_ecr_lin_relu_kernel(
             activate(e, h)
 
         gates = {}
-        spent = ("raw2_0", "raw2_256", "tok_words1", "raw2_512", "x_bf2", "tok_words2")
+        spent = ("raw2_512", "tok_words1", "x_bf2", "tok_words2", "tok_bytes2", "slot_words0")
         for i, tag in enumerate(spent):
             h, r = i // TOP, ORDER[i % TOP]
             gates[h, r] = keep.tile([P, T], F32, name=f"gate{h}_{r}", tag=tag, align_bytes=64)

from contextlib import ExitStack

import concourse.mybir as mybir
from concourse.masks import make_identity

K, T, E, C, N = 1536, 640, 6, 128, 256
TOP, PAD = 3, 64
S = E * C
P = 128
PACK = 4
PASSES = K // (P * PACK)
HALVES = N // P
FLOPS = 2 * K * N * S

F32 = mybir.dt.float32
BF16 = mybir.dt.bfloat16
I32 = mybir.dt.int32
U32 = mybir.dt.uint32
U16 = mybir.dt.uint16
U8 = mybir.dt.uint8
FP8X4 = mybir.dt.float8_e4m3fn_x4
FP4X4 = mybir.dt.float4_e2m1fn_x4
ACT = mybir.ActivationFunctionType
ALU = mybir.AluOpType

X_CHUNKS = (
    ((0, 640),),
    ((0, 256), (256, 512), (512, 640)),
    ((0, 256), (256, 512), (512, 640)),
)
CASTS = (
    (("s", 0, 0, 256), ("v", 0, 256, 512), ("v", 0, 512, 640)),
    (("s", 0, 0, 256), ("s", 256, 256, 512), ("s", 512, 512, 640)),
    (("s", 0, 0, 256), ("s", 256, 256, 512), ("s", 512, 512, 640)),
)
Q_CHUNKS = (
    ((256, 512), (512, 640), (0, 256)),
    ((0, 256), (256, 512), (512, 640)),
    ((0, 512), (512, 640)),
)
ORDER = (2, 1, 0)
WIDE = 1024
SHIFT_ROWS = ((0, 112),)


def tile_moe_ecr_lin_relu_kernel(
    tc, xT, w_words, w_scales, b, gate, offs, pos1, pos2, pos3, out
):
    nc = tc.nc
    with ExitStack() as ctx:
        keep = ctx.enter_context(tc.tile_pool(name="keep", bufs=1))
        psum = ctx.enter_context(tc.psum_pool(name="psum", bufs=1))

        slot_list = keep.tile([P, S // 16], U16, name="slot_list")
        pos_lists = [keep.tile([P, T // 16], U16, name=f"pos_list{r}") for r in range(TOP)]
        w_plane = keep.tile([P, E * PASSES, N], U8, name="w_plane", align_bytes=64)
        bias = keep.tile([P, HALVES, 8], F32, name="bias")
        x_bf = [keep.tile([P, T, PACK], BF16, name=f"x_bf{a}", align_bytes=64) for a in range(PASSES)]
        tok_words = [keep.tile([P, (WIDE, WIDE, T)[a]], U32, name=f"tok_words{a}", align_bytes=64) for a in range(PASSES)]
        tok_bytes01 = keep.tile([P, WIDE], U8, name="tok_bytes01", align_bytes=64)
        tok_bytes2 = keep.tile([P, T], U8, name="tok_bytes2", align_bytes=64)
        slot_words = [keep.tile([P, S], U32, name=f"slot_words{a}", align_bytes=64) for a in range(PASSES)]
        slot_bytes = [keep.tile([P, S], U8, name=f"slot_bytes{a}", align_bytes=64) for a in range(PASSES)]
        y = [keep.tile([P, S + PAD], F32, name=f"y{h}") for h in range(HALVES)]
        zeros = keep.tile([P, PAD], F32, name="zeros")
        prods = [[keep.tile([P, T], F32, name=f"prod{h}_{r}") for r in range(TOP)] for h in range(HALVES)]
        turned = [keep.tile([P, T], F32, name=f"turned{h}") for h in range(HALVES)]
        ident = keep.tile([P, P], F32, name="ident")
        res = [keep.tile([P, T], F32, name=f"res{h}") for h in range(HALVES)]

        nc.vector.memset(zeros[:], 0.0)
        nc.vector.memset(w_plane[:].rearrange("p g n -> p (g n)").bitcast(I32), 0)
        make_identity(nc, ident[:])
        for h in range(HALVES):
            nc.scalar.activation(y[h][:, S:], zeros[:], ACT.Relu)
        nc.vector.memset(tok_bytes01[:].bitcast(I32), 0)
        nc.vector.memset(tok_bytes2[:].bitcast(I32), 0)
        for a in range(PASSES - 1):
            nc.vector.memset(tok_words[a][:, T:].bitcast(I32), 0)
        nc.vector.memset(slot_bytes[1][:].bitcast(I32), 0)

        raw = {}
        for a in range(PASSES):
            rows = xT[a * P * PACK : (a + 1) * P * PACK, :].rearrange("(p j) t -> p j t", j=PACK)
            for t0, t1 in X_CHUNKS[a]:
                raw[a, t0] = keep.tile([P, PACK, t1 - t0], F32, name=f"raw{a}_{t0}", align_bytes=64)
                nc.sync.dma_start(out=raw[a, t0][:], in_=rows[:, :, t0:t1])
            if a == 0:
                nc.sync.dma_start(slot_list[:], offs)
        for q in range(4):
            nc.sync.dma_start(
                out=w_plane[32 * q : 32 * q + 4, :, :].bitcast(I32),
                in_=w_scales[:, :, 4 * q : 4 * q + 4, :].rearrange("e a q n -> q (e a) n").bitcast(I32),
            )
        nc.sync.dma_start(out=bias[:, :, 0:E], in_=b.rearrange("(h p) e -> p h e", p=P))
        w_codes = {}

        def load_weights(a, e0, e1, tag):
            codes = keep.tile([P, e1 - e0, 2 * N], U8, name=f"w_codes{a}_{e0}", tag=tag, align_bytes=64)
            nc.sync.dma_start(
                out=codes[:].bitcast(I32),
                in_=w_words[e0:e1, a, :, :].rearrange("e p c -> p e c").bitcast(I32),
            )
            for e in range(e0, e1):
                w_codes[e, a] = codes[:, e - e0, :]

        load_weights(0, 0, E, "w_codes0")
        load_weights(1, 0, E, "w_codes1")
        for r in ORDER:
            nc.sync.dma_start(pos_lists[r][:], (pos1, pos2, pos3)[r])

        def cast(a):
            for eng, t0, lo, hi in CASTS[a]:
                dst = x_bf[a][:, lo:hi, :].rearrange("p (c i) j -> p c j i", i=4)
                src = raw[a, t0][:, :, lo - t0 : hi - t0].rearrange("p j (c i) -> p c j i", i=4)
                if eng == "s":
                    nc.scalar.activation(dst, src, ACT.Copy)
                else:
                    nc.vector.tensor_copy(dst, src)

        def quantize(a):
            for t0, t1 in Q_CHUNKS[a]:
                plane = (tok_bytes01[:, t0:t1], tok_bytes01[4:, t0:t1], tok_bytes2[:, t0:t1])[a]
                nc.vector.quantize_mx(
                    out=tok_words[a][:, t0:t1].bitcast(FP8X4),
                    scales=plane,
                    in_=x_bf[a][:, t0:t1, :].rearrange("p t j -> p (t j)"),
                )

        def gather(dst, window, e0, e1):
            nc.vector.tensor_copy(
                dst[:, e0 * C : e1 * C], window[:].indirect(slot_list[:, e0 * C // 16 : e1 * C // 16])
            )

        acc = {}

        def multiply(e, h, a):
            if a == 0:
                acc[e, h] = psum.tile([P, C], F32, name=f"acc{e}_{h}", tag=f"bank{(h * E + e) % 8}")
            cols = slice(e * C, (e + 1) * C)
            nc.tensor.matmul_mx(
                out=acc[e, h][:],
                lhsT=w_codes[e, a][:, h * 2 * P : (h + 1) * 2 * P].bitcast(FP4X4),
                lhsT_scale=w_plane[:, e * PASSES + a, h * P : (h + 1) * P],
                rhs=slot_words[a][:, cols].bitcast(FP8X4),
                rhs_scale=slot_bytes[a][:, cols],
                start=(a == 0),
                stop=(a == PASSES - 1),
            )

        def activate(e, h):
            nc.scalar.activation(
                y[h][:, e * C : (e + 1) * C], acc[e, h][:], ACT.Relu, bias=bias[:, h, e : e + 1]
            )

        early = [(e, 0) for e in range(E)] + [(0, 1), (1, 1)]
        late = [(e, 1) for e in range(2, E)]

        cast(0)
        quantize(0)
        gather(slot_words[0], tok_words[0], 0, E)
        cast(1)
        quantize(1)
        gather(slot_bytes[0], tok_bytes01, 0, E)
        gather(slot_words[1], tok_words[1], 0, E)
        cast(2)
        for p0, p1 in SHIFT_ROWS:
            nc.scalar.dma_start(
                out=slot_bytes[1][p0:p1, :].bitcast(I32),
                in_=slot_bytes[0][p0 + 4 : p1 + 4, :].bitcast(I32),
            )
        load_weights(2, 0, 3, "tok_bytes01")
        load_weights(2, 3, E, "raw2_256")
        quantize(2)
        for a in range(PASSES - 1):
            for e, h in early:
                multiply(e, h, a)
        for e0, e1 in ((0, 3), (3, 5), (5, 6)):
            gather(slot_words[2], tok_words[2], e0, e1)
            gather(slot_bytes[2], tok_bytes2, e0, e1)
            for e in range(e0, e1):
                multiply(e, 0, 2)
                activate(e, 0)
        for e in range(2):
            multiply(e, 1, 2)
            activate(e, 1)
        for e, h in late:
            for a in range(PASSES):
                multiply(e, h, a)
            activate(e, h)

        gates = {}
        spent = ("raw2_512", "tok_words1", "x_bf2", "tok_words2", "tok_bytes2", "slot_words0")
        for i, tag in enumerate(spent):
            h, r = i // TOP, ORDER[i % TOP]
            gates[h, r] = keep.tile([P, T], F32, name=f"gate{h}_{r}", tag=tag, align_bytes=64)
            nc.sync.dma_start(out=gates[h, r][:], in_=gate[r, h * P : (h + 1) * P, :])

        def fetch(h, r, t0, t1):
            nc.vector.tensor_tensor(
                prods[h][r][:, t0:t1],
                y[h][:].indirect(pos_lists[r][:, t0 // 16 : t1 // 16]),
                gates[h, r][:, t0:t1],
                ALU.mult,
            )

        blocks = T // P
        sums = {}

        def turn_add(h, r, last):
            for i in range(blocks):
                if r == ORDER[0]:
                    sums[h, i] = psum.tile([P, P], F32, name=f"sum{h}_{i}", tag=f"bank{(4 + i) % 8}")
                nc.tensor.matmul(
                    sums[h, i][:], prods[h][r][:, i * P : (i + 1) * P], ident[:],
                    start=(r == ORDER[0]), stop=last, is_transpose=True,
                )
                if last:
                    nc.scalar.activation(turned[h][:, i * P : (i + 1) * P], sums[h, i][:], ACT.Copy)

        pieces = ((0, 384), (384, T))

        def turn_back(h):
            back = []
            for k, (t0, t1) in enumerate(pieces):
                bank = psum.tile([P, t1 - t0], F32, name=f"back{h}_{k}", tag=f"bank{1 + k}")
                for i in range(t0 // P, t1 // P):
                    nc.tensor.transpose(bank[:, i * P - t0 : (i + 1) * P - t0], turned[h][:, i * P : (i + 1) * P], ident[:])
                back.append(bank)
            return back

        for r in ORDER:
            fetch(0, r, 0, T)
            turn_add(0, r, r == ORDER[-1])
        back = turn_back(0)
        for k, (t0, t1) in enumerate(pieces):
            nc.scalar.activation(res[0][:, t0:t1], back[k][:], ACT.Copy)
        nc.sync.dma_start(out=out[0:P, :], in_=res[0][:])

        fetch(1, ORDER[0], 0, T)
        fetch(1, ORDER[1], 0, T)
        fetch(1, ORDER[2], *pieces[0])
        nc.vector.tensor_tensor(turned[1][:], prods[1][ORDER[0]][:], prods[1][ORDER[1]][:], ALU.add)
        fetch(1, ORDER[2], *pieces[1])
        for t0, t1 in pieces:
            nc.vector.tensor_tensor(res[1][:, t0:t1], prods[1][ORDER[2]][:, t0:t1], turned[1][:, t0:t1], ALU.add)
            nc.sync.dma_start(out=out[P : 2 * P, t0:t1], in_=res[1][:, t0:t1])
